import numpy as np
import ml_dtypes

BF16 = ml_dtypes.bfloat16


def bf(x):
    return np.asarray(x, np.float32).astype(BF16)


def f32(x):
    return np.asarray(x, np.float32)


def f64(x):
    return np.asarray(x).astype(np.float64)


def striped(idx):
    return np.concatenate([l.reshape(-1, 16).T for l in idx])


def rows(idx, k):
    return np.tile(np.repeat(idx, 16, axis=0), (k // (16 * 8), 1))


def look(tab, idx):
    return np.take_along_axis(f64(tab), rows(idx, len(tab)), axis=1)


K, S, V, N, M = 256, 2048, 1024, 1024, 256


def setup_inputs():
    return {"tab": f32(np.random.standard_normal((2, K, S))), "y": f32(np.random.standard_normal((K, V))), "w": bf(np.random.standard_normal((K, M)) / np.sqrt(K)), "b": f32(0.5 * np.random.standard_normal((M, 1))), "offs": striped(np.stack([np.random.permutation(S)[:N] for _ in range(8)]))}


def reference(tab, y, w, b, offs):
    idx = np.stack([g.T.reshape(-1) for g in np.split(offs, 8)])
    x = (look(tab[0], idx) + f64(y)) * (1.0 / (1.0 + np.exp(-look(tab[1], idx))))
    return np.maximum(f64(w).T @ x + f64(b), 0.0)

@@ -1,0 +1,74 @@
+import concourse.mybir as mybir
+
+F32, BF16, U16 = mybir.dt.float32, mybir.dt.bfloat16, mybir.dt.uint16
+ADD, MULT, MAX = mybir.AluOpType.add, mybir.AluOpType.mult, mybir.AluOpType.max
+SIGMOID, RELU = mybir.ActivationFunctionType.Sigmoid, mybir.ActivationFunctionType.Relu
+
+P = 128
+K, S = 256, 2048
+N = 1024
+M = 256
+PIECE = 512
+BLOCKS, PIECES, OUT_BLOCKS = K // P, N // PIECE, M // P
+FLOPS = 2 * K * M * N
+
+
+def tile_lookup_vg_addsig_relu_kernel(tc, tab, y, w, b, offs, out):
+    nc = tc.nc
+    with (
+        tc.tile_pool(name="held", bufs=1) as held,
+        tc.tile_pool(name="work", bufs=4) as work,
+        tc.psum_pool(name="psum", bufs=1) as psum,
+    ):
+        offsets = held.tile([P, N // 16], U16, name="offsets")
+        nc.sync.dma_start(offsets[:], offs)
+
+        gates, values, streams = [], [], []
+        for k in range(BLOCKS):
+            rows = slice(k * P, (k + 1) * P)
+            gate = held.tile([P, S], F32, name=f"gate{k}")
+            value = held.tile([P, S], F32, name=f"value{k}")
+            stream = held.tile([P, N], F32, name=f"stream{k}")
+            nc.sync.dma_start(gate[:], tab[1, rows, :])
+            nc.sync.dma_start(stream[:], y[rows, :])
+            nc.sync.dma_start(value[:], tab[0, rows, :])
+            gates.append(gate)
+            values.append(value)
+            streams.append(stream)
+
+        weights = held.tile([P, BLOCKS, M], BF16, name="weights")
+        nc.gpsimd.dma_start(weights[:], w.rearrange("(k p) m -> p k m", p=P))
+        bias = held.tile([P, OUT_BLOCKS], F32, name="bias")
+        with nc.allow_non_contiguous_dma(reason="256 single values, one to a partition"):
+            nc.gpsimd.dma_start(bias[:], b.rearrange("(o p) u -> p (o u)", p=P))
+
+        sums = {}
+        for c in range(PIECES):
+            for o in range(OUT_BLOCKS):
+                sums[c, o] = psum.tile([P, PIECE], F32, name=f"sum{c}{o}")
+
+        for k in range(BLOCKS):
+            for c in range(PIECES):
+                columns = slice(c * PIECE, (c + 1) * PIECE)
+                picks = offsets[:, c * PIECE // 16 : (c + 1) * PIECE // 16]
+                opened = work.tile([P, PIECE], F32, name="opened")
+                nc.scalar.activation(opened[:], gates[k][:].indirect(picks), SIGMOID)
+                added = work.tile([P, PIECE], F32, name="added")
+                nc.vector.tensor_tensor(added[:], values[k][:].indirect(picks), streams[k][:, columns], ADD)
+                x = work.tile([P, PIECE], BF16, name="x")
+                nc.vector.tensor_tensor(x[:], added[:], opened[:], MULT)
+                for o in range(OUT_BLOCKS):
+                    nc.tensor.matmul(
+                        sums[c, o][:],
+                        weights[:, k, o * P : (o + 1) * P],
+                        x[:],
+                        start=k == 0,
+                        stop=k == BLOCKS - 1,
+                    )
+                    if k == BLOCKS - 1:
+                        result = work.tile([P, PIECE], F32, name=f"result{o}")
+                        if o == 0:
+                            nc.scalar.activation(result[:], sums[c, o][:], RELU, bias=bias[:, o : o + 1])
+                        else:
+                            nc.vector.tensor_scalar(result[:], sums[c, o][:], bias[:, o : o + 1], 0.0, ADD, MAX)
+                        nc.sync.dma_start(out[o * P : (o + 1) * P, columns], result[:])

@@ -9,6 +9,7 @@ K, S = 256, 2048
 N = 1024
 M = 256
 PIECE = 512
+HALF = PIECE // 2
 BLOCKS, PIECES, OUT_BLOCKS = K // P, N // PIECE, M // P
 FLOPS = 2 * K * M * N
 
@@ -17,58 +18,58 @@ def tile_lookup_vg_addsig_relu_kernel(tc, tab, y, w, b, offs, out):
     nc = tc.nc
     with (
         tc.tile_pool(name="held", bufs=1) as held,
-        tc.tile_pool(name="work", bufs=4) as work,
+        tc.tile_pool(name="work", bufs=2) as work,
         tc.psum_pool(name="psum", bufs=1) as psum,
     ):
         offsets = held.tile([P, N // 16], U16, name="offsets")
-        nc.sync.dma_start(offsets[:], offs)
-
-        gates, values, streams = [], [], []
-        for k in range(BLOCKS):
-            rows = slice(k * P, (k + 1) * P)
-            gate = held.tile([P, S], F32, name=f"gate{k}")
-            value = held.tile([P, S], F32, name=f"value{k}")
-            stream = held.tile([P, N], F32, name=f"stream{k}")
-            nc.sync.dma_start(gate[:], tab[1, rows, :])
-            nc.sync.dma_start(stream[:], y[rows, :])
-            nc.sync.dma_start(value[:], tab[0, rows, :])
-            gates.append(gate)
-            values.append(value)
-            streams.append(stream)
-
+        gates = [held.tile([P, S], F32, name=f"gate{k}") for k in range(BLOCKS)]
+        values = [held.tile([P, S], F32, name=f"value{k}") for k in range(BLOCKS)]
+        streams = [[held.tile([P, PIECE], F32, name=f"stream{k}{c}") for c in range(PIECES)] for k in range(BLOCKS)]
         weights = held.tile([P, BLOCKS, M], BF16, name="weights")
-        nc.gpsimd.dma_start(weights[:], w.rearrange("(k p) m -> p k m", p=P))
         bias = held.tile([P, OUT_BLOCKS], F32, name="bias")
+
+        def load_stream(k, c):
+            nc.sync.dma_start(streams[k][c][:], y[k * P : (k + 1) * P, c * PIECE : (c + 1) * PIECE])
+
+        nc.sync.dma_start(offsets[:], offs)
+        nc.sync.dma_start(gates[0][:], tab[1, 0:P, :])
+        nc.sync.dma_start(values[0][:], tab[0, 0:P, :])
+        load_stream(0, 0)
+        load_stream(0, 1)
+        nc.sync.dma_start(weights[:], w.rearrange("(k p) m -> p k m", p=P))
+        nc.sync.dma_start(values[1][:], tab[0, P : 2 * P, :])
+        load_stream(1, 0)
+        nc.sync.dma_start(gates[1][:], tab[1, P : 2 * P, :])
+        load_stream(1, 1)
         with nc.allow_non_contiguous_dma(reason="256 single values, one to a partition"):
-            nc.gpsimd.dma_start(bias[:], b.rearrange("(o p) u -> p (o u)", p=P))
+            nc.sync.dma_start(bias[:], b.rearrange("(o p) u -> p (o u)", p=P))
 
         sums = {}
-        for c in range(PIECES):
+        for h in range(N // HALF):
             for o in range(OUT_BLOCKS):
-                sums[c, o] = psum.tile([P, PIECE], F32, name=f"sum{c}{o}")
+                sums[h, o] = psum.tile([P, HALF], F32, name=f"sum{h}{o}")
 
         for k in range(BLOCKS):
+            last = k == BLOCKS - 1
             for c in range(PIECES):
-                columns = slice(c * PIECE, (c + 1) * PIECE)
                 picks = offsets[:, c * PIECE // 16 : (c + 1) * PIECE // 16]
+                added = work.tile([P, PIECE], F32, name="added")
+                nc.vector.tensor_tensor(added[:], values[k][:].indirect(picks), streams[k][c][:], ADD)
                 opened = work.tile([P, PIECE], F32, name="opened")
                 nc.scalar.activation(opened[:], gates[k][:].indirect(picks), SIGMOID)
-                added = work.tile([P, PIECE], F32, name="added")
-                nc.vector.tensor_tensor(added[:], values[k][:].indirect(picks), streams[k][:, columns], ADD)
                 x = work.tile([P, PIECE], BF16, name="x")
-                nc.vector.tensor_tensor(x[:], added[:], opened[:], MULT)
-                for o in range(OUT_BLOCKS):
-                    nc.tensor.matmul(
-                        sums[c, o][:],
-                        weights[:, k, o * P : (o + 1) * P],
-                        x[:],
-                        start=k == 0,
-                        stop=k == BLOCKS - 1,
-                    )
-                    if k == BLOCKS - 1:
-                        result = work.tile([P, PIECE], F32, name=f"result{o}")
-                        if o == 0:
-                            nc.scalar.activation(result[:], sums[c, o][:], RELU, bias=bias[:, o : o + 1])
-                        else:
-                            nc.vector.tensor_scalar(result[:], sums[c, o][:], bias[:, o : o + 1], 0.0, ADD, MAX)
-                        nc.sync.dma_start(out[o * P : (o + 1) * P, columns], result[:])
+                results = [work.tile([P, PIECE], F32, name=f"result{o}") for o in range(OUT_BLOCKS)] if last else []
+                for half in range(2):
+                    columns = slice(half * HALF, (half + 1) * HALF)
+                    nc.vector.tensor_tensor(x[:, columns], added[:, columns], opened[:, columns], MULT)
+                    for o in range(OUT_BLOCKS):
+                        total = sums[2 * c + half, o]
+                        nc.tensor.matmul(
+                            total[:], weights[:, k, o * P : (o + 1) * P], x[:, columns], start=k == 0, stop=last
+                        )
+                        if last and o == 0:
+                            nc.scalar.activation(results[o][:, columns], total[:], RELU, bias=bias[:, o : o + 1])
+                        elif last:
+                            nc.vector.tensor_scalar(results[o][:, columns], total[:], bias[:, o : o + 1], 0.0, ADD, MAX)
+                for o in range(len(results)):
+                    nc.sync.dma_start(out[o * P : (o + 1) * P, c * PIECE : (c + 1) * PIECE], results[o][:])

import concourse.mybir as mybir

F32, BF16, U16 = mybir.dt.float32, mybir.dt.bfloat16, mybir.dt.uint16
ADD, MULT, MAX = mybir.AluOpType.add, mybir.AluOpType.mult, mybir.AluOpType.max
SIGMOID, RELU = mybir.ActivationFunctionType.Sigmoid, mybir.ActivationFunctionType.Relu

P = 128
K, S = 256, 2048
N = 1024
M = 256
PIECE = 512
HALF = PIECE // 2
BLOCKS, PIECES, OUT_BLOCKS = K // P, N // PIECE, M // P
FLOPS = 2 * K * M * N


def tile_lookup_vg_addsig_relu_kernel(tc, tab, y, w, b, offs, out):
    nc = tc.nc
    with (
        tc.tile_pool(name="held", bufs=1) as held,
        tc.tile_pool(name="work", bufs=2) as work,
        tc.psum_pool(name="psum", bufs=1) as psum,
    ):
        offsets = held.tile([P, N // 16], U16, name="offsets")
        gates = [held.tile([P, S], F32, name=f"gate{k}") for k in range(BLOCKS)]
        values = [held.tile([P, S], F32, name=f"value{k}") for k in range(BLOCKS)]
        streams = [[held.tile([P, PIECE], F32, name=f"stream{k}{c}") for c in range(PIECES)] for k in range(BLOCKS)]
        weights = held.tile([P, BLOCKS, M], BF16, name="weights")
        bias = held.tile([P, OUT_BLOCKS], F32, name="bias")

        def load_stream(k, c):
            nc.sync.dma_start(streams[k][c][:], y[k * P : (k + 1) * P, c * PIECE : (c + 1) * PIECE])

        nc.sync.dma_start(offsets[:], offs)
        nc.sync.dma_start(gates[0][:], tab[1, 0:P, :])
        nc.sync.dma_start(values[0][:], tab[0, 0:P, :])
        load_stream(0, 0)
        load_stream(0, 1)
        nc.sync.dma_start(weights[:], w.rearrange("(k p) m -> p k m", p=P))
        nc.sync.dma_start(values[1][:], tab[0, P : 2 * P, :])
        load_stream(1, 0)
        nc.sync.dma_start(gates[1][:], tab[1, P : 2 * P, :])
        load_stream(1, 1)
        with nc.allow_non_contiguous_dma(reason="256 single values, one to a partition"):
            nc.sync.dma_start(bias[:], b.rearrange("(o p) u -> p (o u)", p=P))

        sums = {}
        for h in range(N // HALF):
            for o in range(OUT_BLOCKS):
                sums[h, o] = psum.tile([P, HALF], F32, name=f"sum{h}{o}")

        for k in range(BLOCKS):
            last = k == BLOCKS - 1
            for c in range(PIECES):
                picks = offsets[:, c * PIECE // 16 : (c + 1) * PIECE // 16]
                added = work.tile([P, PIECE], F32, name="added")
                nc.vector.tensor_tensor(added[:], values[k][:].indirect(picks), streams[k][c][:], ADD)
                opened = work.tile([P, PIECE], F32, name="opened")
                nc.scalar.activation(opened[:], gates[k][:].indirect(picks), SIGMOID)
                x = work.tile([P, PIECE], BF16, name="x")
                results = [work.tile([P, PIECE], F32, name=f"result{o}") for o in range(OUT_BLOCKS)] if last else []
                for half in range(2):
                    columns = slice(half * HALF, (half + 1) * HALF)
                    nc.vector.tensor_tensor(x[:, columns], added[:, columns], opened[:, columns], MULT)
                    for o in range(OUT_BLOCKS):
                        total = sums[2 * c + half, o]
                        nc.tensor.matmul(
                            total[:], weights[:, k, o * P : (o + 1) * P], x[:, columns], start=k == 0, stop=last
                        )
                        if last and o == 0:
                            nc.scalar.activation(results[o][:, columns], total[:], RELU, bias=bias[:, o : o + 1])
                        elif last:
                            nc.vector.tensor_scalar(results[o][:, columns], total[:], bias[:, o : o + 1], 0.0, ADD, MAX)
                for o in range(len(results)):
                    nc.sync.dma_start(out[o * P : (o + 1) * P, c * PIECE : (c + 1) * PIECE], results[o][:])
